import numpy as np
import ml_dtypes


def mxq(x, axis, fmt="e4m3"):
    dtype, down = {"e4m3": (ml_dtypes.float8_e4m3fn, 7), "e5m2": (ml_dtypes.float8_e5m2, 14)}[fmt]
    v = np.moveaxis(np.asarray(x, np.float32).astype(ml_dtypes.bfloat16).astype(np.float64), axis, -1)
    blocks = v.reshape(v.shape[:-1] + (-1, 32))
    amax = np.abs(blocks).max(-1, keepdims=True)
    byte = np.maximum(np.where(amax > 0, np.frexp(amax)[1] - 1 + 127, 0) - down, 1)
    scale = np.exp2(byte - 127.0)
    codes = (blocks / scale).astype(np.float32).astype(dtype).astype(np.float64)
    return np.moveaxis((codes * scale).reshape(v.shape), -1, axis)


WIDE = False


def mx_kscale(k):
    if not WIDE:
        return np.ones(k)
    levels = np.array([10, -10, 5, -5, 0])
    if k % 512:
        return np.exp2(np.random.permutation(np.resize(levels, k // 32))).repeat(32)
    a = np.empty((k // 512, 16))
    for p in range(k // 512):
        a[p, :8] = np.random.permutation(np.resize(levels, 8))
        for g in range(8):
            far = levels[np.abs(levels - a[p, g]) >= 10]
            a[p, g + 8] = far[np.random.randint(len(far))]
    return np.exp2(a.ravel()).repeat(32)


def f64(x):
    return np.asarray(x).astype(np.float64)


def striped(idx):
    return np.tile(idx.reshape(-1, 16).T, (8, 1)).astype(np.uint16)


def unstriped(offs):
    return offs[:16].T.reshape(-1).astype(np.int64)


def striped8(idx):
    return np.concatenate([x.reshape(-1, 16).T for x in idx]).astype(np.uint16)


def runs(offs, k):
    lists = np.stack([offs[16 * r : 16 * r + 16].T.reshape(-1) for r in range(8)]).astype(np.int64)
    return lists[np.arange(k) % 512 // 64]


def pack_weight(w):
    k, n = w.shape
    w = f64(np.asarray(w, np.float32).astype(ml_dtypes.bfloat16)).reshape(k // 32, 32, n)
    amax = np.abs(w).max(1)
    byte = np.clip(np.where(amax > 0, np.frexp(amax)[1] - 1 + 127 - 7, 1), 1, 254)
    scaled = (w * np.exp2(127.0 - byte)[:, None, :]).reshape(k, n).astype(np.float32)
    words = np.ascontiguousarray(scaled.reshape(k // 512, 128, 4, n).transpose(0, 1, 3, 2)).astype(ml_dtypes.float8_e4m3fn).view(np.uint8)
    return words, np.ascontiguousarray(byte.astype(np.uint8).reshape(k // 512, 16, n))


def unpack_weight(words, scales):
    g, p, n, _ = words.shape
    vals = np.ascontiguousarray(words).view(ml_dtypes.float8_e4m3fn).astype(np.float64) * np.repeat(np.exp2(scales.astype(np.float64) - 127.0), 8, axis=1)[..., None]
    return vals.transpose(0, 1, 3, 2).reshape(g * 512, n)


K, T, S, H, C, U = 512, 2048, 256, 512, 512, 512


def setup_inputs():
    n = np.random.standard_normal
    s = mx_kscale(K)[:, None]
    packed_xT = pack_weight(n((K, T)) * s)
    packed_w1 = pack_weight(n((K, H)) / np.sqrt(2 * K) / s)
    packed_w2 = pack_weight(n((K, H)) / np.sqrt(2 * K) / s)
    perm = np.random.permutation(U)
    return {
        "x_words": packed_xT[0],
        "x_scales": packed_xT[1],
        "w1_words": packed_w1[0],
        "w1_scales": packed_w1[1],
        "w2_words": packed_w2[0],
        "w2_scales": packed_w2[1],
        "tau": np.random.uniform(0.3, 0.9, (H, 1)).astype(np.float32),
        "gs": (np.random.uniform(0.5, 1.5, (K, 1)) / s).astype(np.float32),
        "offs": striped(np.random.permutation(T)[:S]),
        "hz": striped8(np.random.randint(0, T, (8, S))),
        "n1": striped(np.random.permutation(S)),
        "n2": striped(np.random.permutation(S)),
        "cand": striped(np.random.permutation(T)[:C]),
        "n3": striped(perm[:S]),
        "n4": striped(perm[S:]),
        "n5": striped(np.random.permutation(S)),
    }


def reference(x_words, x_scales, w1_words, w1_scales, w2_words, w2_scales, tau, gs, offs, hz, n1, n2, cand, n3, n4, n5):
    x_cand = unpack_weight(x_words, x_scales)[:, unstriped(cand)]
    xq = unpack_weight(x_words, x_scales)[:, unstriped(offs)]
    x_hz = unpack_weight(x_words, x_scales)[np.arange(K)[:, None], runs(hz, K)]
    y = unpack_weight(w1_words, w1_scales).T @ xq + unpack_weight(w2_words, w2_scales).T @ x_hz
    top = y.max(axis=1, keepdims=True)
    ea = np.exp(f64(tau) * (y[:, unstriped(n1)] - top))
    sm = y * ea
    ds = np.zeros((H, S))
    ds[:, unstriped(n2)] = sm
    z = f64(gs) * (2.0 * ds - (0.5 * y))
    s = 0.0625 * ((x_cand.T @ mxq(z, 0, "e4m3")))
    nw = s - s[:, unstriped(n5)]
    ph = np.zeros((C, U))
    ph[:, unstriped(n3)] = s
    out = ph.copy()
    out[:, unstriped(n4)] = nw
    return out

@@ -1,0 +1,221 @@
+from contextlib import ExitStack
+
+import concourse.mybir as mybir
+
+F32 = mybir.dt.float32
+BF16 = mybir.dt.bfloat16
+I32 = mybir.dt.int32
+U32 = mybir.dt.uint32
+U16 = mybir.dt.uint16
+U8 = mybir.dt.uint8
+FP8X4 = mybir.dt.float8_e4m3fn_x4
+ALU = mybir.AluOpType
+ACT = mybir.ActivationFunctionType
+
+P = 128
+PACK = 4
+K, T, S, H, C, U = 512, 2048, 256, 512, 512, 512
+HALF = S // 2
+FLOPS = 2 * (2 * K * H * S + K * C * S)
+
+
+def tile_picked_thcesdpagq_none_p_kernel(
+    tc, x_words, x_scales, w1_words, w1_scales, w2_words, w2_scales, tau, gs, offs, hz, n1, n2, cand, n3, n4, n5, out
+):
+    nc = tc.nc
+    with ExitStack() as ctx:
+        lists = ctx.enter_context(tc.tile_pool(name="lists", bufs=1))
+        keep = ctx.enter_context(tc.tile_pool(name="keep", bufs=1))
+        psum = ctx.enter_context(tc.psum_pool(name="psum", bufs=1))
+
+        def load_list(src, name):
+            tile = lists.tile(list(src.shape), U16, name=name)
+            nc.sync.dma_start(tile[:], src)
+            return tile
+
+        def words_of(src):
+            return src[0].rearrange("p n t -> p (n t)").bitcast(I32)
+
+        def bank(index, width):
+            return psum.tile([P, width], F32, name="bank%d" % index, tag="bank%d" % index)
+
+        xs_win = keep.tile([P, T], U8, name="xs_win")
+        x_win = keep.tile([P, T], U32, name="x_win")
+        w1_raw = keep.tile([P, H], U32, name="w1_raw")
+        w2_raw = keep.tile([P, H], U32, name="w2_raw")
+        ws_raw = keep.tile([P, 2, H], U8, name="ws_raw")
+        tau_t = keep.tile([P, PACK], F32, name="tau_t")
+        gs_t = keep.tile([P, PACK], F32, name="gs_t")
+        hz_l = load_list(hz, "hz_l")
+        offs_l = load_list(offs, "offs_l")
+        nc.scalar.dma_start(
+            xs_win[:].bitcast(I32), x_scales[0].bitcast(I32).unsqueeze(1).broadcast_to([16, 8, T // 4])
+        )
+        nc.scalar.dma_start(tau_t[:], tau.rearrange("(p t) o -> p (t o)", t=PACK))
+        nc.scalar.dma_start(x_win[:].bitcast(I32), words_of(x_words))
+        nc.scalar.dma_start(w1_raw[:].bitcast(I32), words_of(w1_words))
+        nc.scalar.dma_start(w2_raw[:].bitcast(I32), words_of(w2_words))
+        for q in range(4):
+            for i, src in enumerate((w1_scales, w2_scales)):
+                rows = src[0, 4 * q : 4 * q + 4, :].bitcast(I32)
+                queue = nc.gpsimd if q == 0 else nc.sync
+                queue.dma_start(
+                    ws_raw[32 * q : 32 * q + 32, i, :].bitcast(I32), rows.unsqueeze(0).broadcast_to([8, 4, H // 4])
+                )
+        nc.gpsimd.dma_start(gs_t[:], gs.rearrange("(p t) o -> p (t o)", t=PACK))
+
+        def gather_packed(dst, window, offsets):
+            nc.vector.tensor_copy(dst, window[:].indirect(offsets))
+
+        def place_scale_rows(got, width, name, queue):
+            plane = keep.tile([P, width], U8, name=name, align_bytes=64)
+            nc.vector.tensor_copy(plane[:].bitcast(I32), got[:].bitcast(I32))
+            for r in range(1, 4):
+                queue.dma_start(plane[r:P:32, :].bitcast(I32), got[8 * r : P : 32, :].bitcast(I32))
+            return plane
+
+        tau_neg = keep.tile([P, PACK], F32, name="tau_neg")
+        nc.scalar.activation(tau_neg[:], tau_t[:], ACT.Copy, scale=-1.0)
+
+        tok_bytes = keep.tile([P, 2 * S], U8, name="tok_bytes")
+        gather_packed(tok_bytes[:, 0:S], xs_win, hz_l[:])
+        gather_packed(tok_bytes[:, S : 2 * S], xs_win, offs_l[:])
+        tok_plane = place_scale_rows(tok_bytes, 2 * S, "tok_plane", nc.scalar)
+
+        n1_l = load_list(n1, "n1_l")
+        cand_l = load_list(cand, "cand_l")
+        n2_l = load_list(n2, "n2_l")
+
+        gs2 = keep.tile([P, PACK], F32, name="gs2")
+        gs_half = keep.tile([P, PACK], F32, name="gs_half")
+
+        ws = keep.tile([P, 2, PACK, P], U8, name="ws", align_bytes=64)
+        w1 = keep.tile([P, PACK, P], U32, name="w1", align_bytes=64)
+        w2 = keep.tile([P, PACK, P], U32, name="w2", align_bytes=64)
+
+        for i in range(2):
+            nc.vector.tensor_copy(
+                ws[:, i, :, :].rearrange("p t m -> p m t"), ws_raw[:, i, :].rearrange("p (m t) -> p m t", t=PACK)
+            )
+
+        def deal(copy, dealt, raw, lo, hi):
+            copy(dealt[:].rearrange("p t m -> p m t")[:, lo:hi, :], raw[:].rearrange("p (m t) -> p m t", t=PACK)[:, lo:hi, :])
+
+        deal(nc.scalar.copy, w1, w1_raw, 0, P)
+        deal(nc.scalar.copy, w2, w2_raw, 0, P // 2)
+
+        offs_words = keep.tile([P, S], U32, name="offs_words", align_bytes=64)
+        hz_words = keep.tile([P, S], U32, name="hz_words", align_bytes=64)
+        gather_packed(offs_words[:], x_win, offs_l[:])
+        gather_packed(hz_words[:], x_win, hz_l[:])
+        deal(nc.vector.tensor_copy, w2, w2_raw, P // 2, P)
+
+        n5_l = load_list(n5, "n5_l")
+        n3_l = load_list(n3, "n3_l")
+        n4_l = load_list(n4, "n4_l")
+
+        top = keep.tile([P, PACK], F32, name="top")
+        bias = keep.tile([P, PACK], F32, name="bias")
+        z = keep.tile([P, S, PACK], BF16, name="z", align_bytes=64)
+        cand_words = keep.tile([P, C], U32, name="cand_words", align_bytes=64)
+        ys, eas, dss, yhs = [], [], [], []
+
+        def project(t):
+            acc = bank(t, S)
+            nc.tensor.matmul_mx(
+                out=acc[:], lhsT=w1[:, t, :].bitcast(FP8X4), lhsT_scale=ws[:, 0, t, :],
+                rhs=offs_words[:].bitcast(FP8X4), rhs_scale=tok_plane[:, S : 2 * S], start=True, stop=False,
+            )
+            nc.tensor.matmul_mx(
+                out=acc[:], lhsT=w2[:, t, :].bitcast(FP8X4), lhsT_scale=ws[:, 1, t, :],
+                rhs=hz_words[:].bitcast(FP8X4), rhs_scale=tok_plane[:, 0:S], start=False, stop=True,
+            )
+            y = keep.tile([P, 2 * S], F32, name="y%d" % t)
+            nc.vector.tensor_scalar(y[:, 0:S], acc[:], 1.0, None, ALU.mult, ALU.max, accum_out=top[:, t : t + 1])
+            nc.vector.tensor_tensor(bias[:, t : t + 1], top[:, t : t + 1], tau_neg[:, t : t + 1], ALU.mult)
+            ea = keep.tile([P, S], F32, name="ea%d" % t)
+            nc.scalar.activation(
+                ea[:], y[:].indirect(n1_l[:]), ACT.Exp, bias=bias[:, t : t + 1], scale=tau_t[:, t : t + 1]
+            )
+            ys.append(y)
+            eas.append(ea)
+
+        def weigh(t, lo, hi):
+            nc.vector.scalar_tensor_tensor(
+                z[:, lo:hi, t], dss[t][:, lo:hi], gs2[:, t : t + 1], yhs[t][:, lo:hi], ALU.mult, ALU.add
+            )
+
+        for t in range(PACK):
+            project(t)
+        for t in range(PACK):
+            sm = keep.tile([P, S], F32, name="sm%d" % t)
+            nc.vector.tensor_tensor(sm[:], ys[t][:, 0:S], eas[t][:], ALU.mult)
+            ds = keep.tile([P, 2 * S], F32, name="ds%d" % t)
+            nc.scalar.activation(ds[:].indirect(n2_l[:]), sm[:], ACT.Copy)
+            dss.append(ds)
+        nc.vector.tensor_scalar(gs2[:], gs_t[:], 2.0, None, ALU.mult)
+        nc.vector.tensor_scalar(gs_half[:], gs_t[:], -0.5, None, ALU.mult)
+        for t in range(PACK):
+            yh = keep.tile([P, S], F32, name="yh%d" % t)
+            nc.vector.tensor_scalar(yh[:], ys[t][:, 0:S], gs_half[:, t : t + 1], None, ALU.mult)
+            yhs.append(yh)
+        cand_bytes = keep.tile([P, C], U8, name="cand_bytes")
+        for lo in range(0, C, S):
+            gather_packed(cand_bytes[:, lo : lo + S], xs_win, cand_l[:, lo // 16 : (lo + S) // 16])
+        cand_plane = place_scale_rows(cand_bytes, C, "cand_plane", nc.sync)
+        for lo in range(0, C, S):
+            gather_packed(cand_words[:, lo : lo + S], x_win, cand_l[:, lo // 16 : (lo + S) // 16])
+        for t in range(PACK - 1):
+            weigh(t, 0, S)
+
+        pages = []
+        for c in range(C // P):
+            page = keep.tile([P, U], F32, name="page%d" % c)
+            pages.append(page)
+
+        z_words = keep.tile([P, S], U32, name="z_words", align_bytes=64)
+        z_plane = keep.tile([P, S], U8, name="z_plane", align_bytes=64)
+        for lo in (0, HALF):
+            weigh(PACK - 1, lo, lo + HALF)
+        for lo in (0, HALF):
+            nc.vector.quantize_mx(
+                out=z_words[:, lo : lo + HALF].bitcast(FP8X4),
+                scales=z_plane[:, lo : lo + HALF],
+                in_=z[:, lo : lo + HALF, :].rearrange("p j t -> p (j t)"),
+            )
+
+        def score(acc, c, lo, hi):
+            nc.tensor.matmul_mx(
+                out=acc[:], lhsT=cand_words[:, c * P : (c + 1) * P].bitcast(FP8X4),
+                lhsT_scale=cand_plane[:, c * P : (c + 1) * P],
+                rhs=z_words[:, lo:hi].bitcast(FP8X4), rhs_scale=z_plane[:, lo:hi], start=True, stop=True,
+            )
+
+        news = []
+
+        def finish(c):
+            nc.scalar.activation(pages[c][:].indirect(n4_l[:]), news[c][:], ACT.Copy)
+            nc.sync.dma_start(out[c * P : (c + 1) * P, :], pages[c][:])
+
+        for c in range(C // P):
+            s = keep.tile([P, S + 16], F32, name="s%d" % c)
+            other = keep.tile([P, S], F32, name="other%d" % c)
+            if c == 0:
+                first, second = bank(4, HALF), bank(5, HALF)
+                score(first, c, 0, HALF)
+                score(second, c, HALF, S)
+                nc.scalar.activation(s[:, 0:HALF], first[:], ACT.Copy, scale=0.0625)
+                nc.scalar.activation(pages[c][:].indirect(n3_l[:, 0 : HALF // 16]), s[:, 0:HALF], ACT.Copy)
+                nc.vector.tensor_scalar(s[:, HALF:S], second[:], 0.0625, None, ALU.mult)
+                nc.scalar.activation(other[:], s[:].indirect(n5_l[:]), ACT.Copy)
+                nc.scalar.activation(pages[c][:].indirect(n3_l[:, HALF // 16 : S // 16]), s[:, HALF:S], ACT.Copy)
+            else:
+                acc = bank((5 + c) % 8, S)
+                score(acc, c, 0, S)
+                nc.vector.tensor_scalar(s[:, 0:S], acc[:], 0.0625, None, ALU.mult)
+                nc.scalar.activation(other[:], s[:].indirect(n5_l[:]), ACT.Copy)
+                nc.scalar.activation(pages[c][:].indirect(n3_l[:]), s[:, 0:S], ACT.Copy)
+            nw = keep.tile([P, S], F32, name="nw%d" % c)
+            nc.vector.tensor_tensor(nw[:], s[:, 0:S], other[:], ALU.subtract)
+            news.append(nw)
+            finish(c)

@@ -89,8 +89,8 @@ def tile_picked_thcesdpagq_none_p_kernel(
         gs2 = keep.tile([P, PACK], F32, name="gs2")
         gs_half = keep.tile([P, PACK], F32, name="gs_half")
 
-        ws = keep.tile([P, 2, PACK, P], U8, name="ws", align_bytes=64)
-        w1 = keep.tile([P, PACK, P], U32, name="w1", align_bytes=64)
+        ws = keep.tile([P, 2, PACK, P], U8, name="ws", tag="bytes_then_cand", align_bytes=64)
+        w1 = keep.tile([P, PACK, P], U32, name="w1", tag="words_then_cand", align_bytes=64)
         w2 = keep.tile([P, PACK, P], U32, name="w2", align_bytes=64)
 
         for i in range(2):
@@ -117,7 +117,6 @@ def tile_picked_thcesdpagq_none_p_kernel(
         top = keep.tile([P, PACK], F32, name="top")
         bias = keep.tile([P, PACK], F32, name="bias")
         z = keep.tile([P, S, PACK], BF16, name="z", align_bytes=64)
-        cand_words = keep.tile([P, C], U32, name="cand_words", align_bytes=64)
         ys, eas, dss, yhs = [], [], [], []
 
         def project(t):
@@ -159,7 +158,8 @@ def tile_picked_thcesdpagq_none_p_kernel(
             yh = keep.tile([P, S], F32, name="yh%d" % t)
             nc.vector.tensor_scalar(yh[:], ys[t][:, 0:S], gs_half[:, t : t + 1], None, ALU.mult)
             yhs.append(yh)
-        cand_bytes = keep.tile([P, C], U8, name="cand_bytes")
+        cand_words = keep.tile([P, C], U32, name="cand_words", tag="words_then_cand", align_bytes=64)
+        cand_bytes = keep.tile([P, C], U8, name="cand_bytes", tag="bytes_then_cand", align_bytes=64)
         for lo in range(0, C, S):
             gather_packed(cand_bytes[:, lo : lo + S], xs_win, cand_l[:, lo // 16 : (lo + S) // 16])
         cand_plane = place_scale_rows(cand_bytes, C, "cand_plane", nc.sync)

@@ -46,32 +46,34 @@ def tile_picked_thcesdpagq_none_p_kernel(
         ws_raw = keep.tile([P, 2, H], U8, name="ws_raw")
         tau_t = keep.tile([P, PACK], F32, name="tau_t")
         gs_t = keep.tile([P, PACK], F32, name="gs_t")
+
+        def spread_rows(src):
+            rows = src[0].bitcast(I32)
+            return rows.unsqueeze(1).broadcast_to([16, 8, rows.shape[1]])
+
+        def place_rows(plane, got, queue):
+            for r in range(1, 4):
+                queue.dma_start(plane[r:P:32, :].bitcast(I32), got[8 * r : P : 32, :].bitcast(I32))
+
         hz_l = load_list(hz, "hz_l")
+        nc.sync.dma_start(tau_t[:], tau.rearrange("(p t) o -> p (t o)", t=PACK))
         offs_l = load_list(offs, "offs_l")
-        nc.scalar.dma_start(
-            xs_win[:].bitcast(I32), x_scales[0].bitcast(I32).unsqueeze(1).broadcast_to([16, 8, T // 4])
-        )
-        nc.scalar.dma_start(tau_t[:], tau.rearrange("(p t) o -> p (t o)", t=PACK))
-        nc.scalar.dma_start(x_win[:].bitcast(I32), words_of(x_words))
-        nc.scalar.dma_start(w1_raw[:].bitcast(I32), words_of(w1_words))
-        nc.scalar.dma_start(w2_raw[:].bitcast(I32), words_of(w2_words))
-        for q in range(4):
-            for i, src in enumerate((w1_scales, w2_scales)):
-                rows = src[0, 4 * q : 4 * q + 4, :].bitcast(I32)
-                queue = nc.gpsimd if q == 0 else nc.sync
-                queue.dma_start(
-                    ws_raw[32 * q : 32 * q + 32, i, :].bitcast(I32), rows.unsqueeze(0).broadcast_to([8, 4, H // 4])
-                )
+        n1_l = load_list(n1, "n1_l")
+        nc.scalar.dma_start(xs_win[:].bitcast(I32), spread_rows(x_scales))
+        for i, src in enumerate((w1_scales, w2_scales)):
+            nc.scalar.dma_start(ws_raw[:, i, :].bitcast(I32), spread_rows(src))
+        nc.sync.dma_start(x_win[:].bitcast(I32), words_of(x_words))
+        nc.sync.dma_start(w1_raw[:].bitcast(I32), words_of(w1_words))
+        nc.sync.dma_start(w2_raw[:].bitcast(I32), words_of(w2_words))
         nc.gpsimd.dma_start(gs_t[:], gs.rearrange("(p t) o -> p (t o)", t=PACK))
 
         def gather_packed(dst, window, offsets):
             nc.vector.tensor_copy(dst, window[:].indirect(offsets))
 
         def place_scale_rows(got, width, name, queue):
-            plane = keep.tile([P, width], U8, name=name, align_bytes=64)
+            plane = keep.tile([P, width], U8, name=name, tag=name, align_bytes=64)
             nc.vector.tensor_copy(plane[:].bitcast(I32), got[:].bitcast(I32))
-            for r in range(1, 4):
-                queue.dma_start(plane[r:P:32, :].bitcast(I32), got[8 * r : P : 32, :].bitcast(I32))
+            place_rows(plane, got, queue)
             return plane
 
         tau_neg = keep.tile([P, PACK], F32, name="tau_neg")
@@ -82,21 +84,24 @@ def tile_picked_thcesdpagq_none_p_kernel(
         gather_packed(tok_bytes[:, S : 2 * S], xs_win, offs_l[:])
         tok_plane = place_scale_rows(tok_bytes, 2 * S, "tok_plane", nc.scalar)
 
-        n1_l = load_list(n1, "n1_l")
-        cand_l = load_list(cand, "cand_l")
-        n2_l = load_list(n2, "n2_l")
-
         gs2 = keep.tile([P, PACK], F32, name="gs2")
         gs_half = keep.tile([P, PACK], F32, name="gs_half")
 
-        ws = keep.tile([P, 2, PACK, P], U8, name="ws", tag="bytes_then_cand", align_bytes=64)
+        ws_dealt = keep.tile([P, 2 * H], U8, name="ws_dealt")
         w1 = keep.tile([P, PACK, P], U32, name="w1", tag="words_then_cand", align_bytes=64)
         w2 = keep.tile([P, PACK, P], U32, name="w2", align_bytes=64)
 
         for i in range(2):
             nc.vector.tensor_copy(
-                ws[:, i, :, :].rearrange("p t m -> p m t"), ws_raw[:, i, :].rearrange("p (m t) -> p m t", t=PACK)
+                ws_dealt[:, i * H : (i + 1) * H].rearrange("p (t m) -> p m t", t=PACK),
+                ws_raw[:, i, :].rearrange("p (m t) -> p m t", t=PACK),
             )
+        ws = place_scale_rows(ws_dealt, 2 * H, "bytes_then_cand", nc.sync)
+        cand_l = load_list(cand, "cand_l")
+        n2_l = load_list(n2, "n2_l")
+        n5_l = load_list(n5, "n5_l")
+        n3_l = load_list(n3, "n3_l")
+        n4_l = load_list(n4, "n4_l")
 
         def deal(copy, dealt, raw, lo, hi):
             copy(dealt[:].rearrange("p t m -> p m t")[:, lo:hi, :], raw[:].rearrange("p (m t) -> p m t", t=PACK)[:, lo:hi, :])
@@ -110,10 +115,6 @@ def tile_picked_thcesdpagq_none_p_kernel(
         gather_packed(hz_words[:], x_win, hz_l[:])
         deal(nc.vector.tensor_copy, w2, w2_raw, P // 2, P)
 
-        n5_l = load_list(n5, "n5_l")
-        n3_l = load_list(n3, "n3_l")
-        n4_l = load_list(n4, "n4_l")
-
         top = keep.tile([P, PACK], F32, name="top")
         bias = keep.tile([P, PACK], F32, name="bias")
         z = keep.tile([P, S, PACK], BF16, name="z", align_bytes=64)
@@ -122,11 +123,11 @@ def tile_picked_thcesdpagq_none_p_kernel(
         def project(t):
             acc = bank(t, S)
             nc.tensor.matmul_mx(
-                out=acc[:], lhsT=w1[:, t, :].bitcast(FP8X4), lhsT_scale=ws[:, 0, t, :],
+                out=acc[:], lhsT=w1[:, t, :].bitcast(FP8X4), lhsT_scale=ws[:, t * P : (t + 1) * P],
                 rhs=offs_words[:].bitcast(FP8X4), rhs_scale=tok_plane[:, S : 2 * S], start=True, stop=False,
             )
             nc.tensor.matmul_mx(
-                out=acc[:], lhsT=w2[:, t, :].bitcast(FP8X4), lhsT_scale=ws[:, 1, t, :],
+                out=acc[:], lhsT=w2[:, t, :].bitcast(FP8X4), lhsT_scale=ws[:, H + t * P : H + (t + 1) * P],
                 rhs=hz_words[:].bitcast(FP8X4), rhs_scale=tok_plane[:, 0:S], start=False, stop=True,
             )
             y = keep.tile([P, 2 * S], F32, name="y%d" % t)
@@ -152,8 +153,8 @@ def tile_picked_thcesdpagq_none_p_kernel(
             ds = keep.tile([P, 2 * S], F32, name="ds%d" % t)
             nc.scalar.activation(ds[:].indirect(n2_l[:]), sm[:], ACT.Copy)
             dss.append(ds)
-        nc.vector.tensor_scalar(gs2[:], gs_t[:], 2.0, None, ALU.mult)
-        nc.vector.tensor_scalar(gs_half[:], gs_t[:], -0.5, None, ALU.mult)
+        nc.gpsimd.tensor_scalar(gs2[:], gs_t[:], 2.0, None, ALU.mult)
+        nc.gpsimd.tensor_scalar(gs_half[:], gs_t[:], -0.5, None, ALU.mult)
         for t in range(PACK):
             yh = keep.tile([P, S], F32, name="yh%d" % t)
             nc.vector.tensor_scalar(yh[:], ys[t][:, 0:S], gs_half[:, t : t + 1], None, ALU.mult)

@@ -16,6 +16,8 @@ P = 128
 PACK = 4
 K, T, S, H, C, U = 512, 2048, 256, 512, 512, 512
 HALF = S // 2
+X_MOVES = ((2, 16), (3, 17))
+W_MOVES = ((1, 8), (2, 16), (3, 24))
 FLOPS = 2 * (2 * K * H * S + K * C * S)
 
 
@@ -46,34 +48,29 @@ def tile_picked_thcesdpagq_none_p_kernel(
         ws_raw = keep.tile([P, 2, H], U8, name="ws_raw")
         tau_t = keep.tile([P, PACK], F32, name="tau_t")
         gs_t = keep.tile([P, PACK], F32, name="gs_t")
-
-        def spread_rows(src):
-            rows = src[0].bitcast(I32)
-            return rows.unsqueeze(1).broadcast_to([16, 8, rows.shape[1]])
-
-        def place_rows(plane, got, queue):
-            for r in range(1, 4):
-                queue.dma_start(plane[r:P:32, :].bitcast(I32), got[8 * r : P : 32, :].bitcast(I32))
+        nc.vector.memset(xs_win[:, 0 : T // 2].bitcast(I32), 0)
+        nc.gpsimd.memset(xs_win[:, T // 2 : T].bitcast(I32), 0)
 
         hz_l = load_list(hz, "hz_l")
         nc.sync.dma_start(tau_t[:], tau.rearrange("(p t) o -> p (t o)", t=PACK))
         offs_l = load_list(offs, "offs_l")
-        n1_l = load_list(n1, "n1_l")
-        nc.scalar.dma_start(xs_win[:].bitcast(I32), spread_rows(x_scales))
         for i, src in enumerate((w1_scales, w2_scales)):
-            nc.scalar.dma_start(ws_raw[:, i, :].bitcast(I32), spread_rows(src))
+            rows = src[0].bitcast(I32).unsqueeze(1).broadcast_to([16, 8, H // 4])
+            nc.scalar.dma_start(ws_raw[:, i, :].bitcast(I32), rows)
+        for r, queue in enumerate((nc.sync, nc.scalar)):
+            queue.dma_start(xs_win[r:P:16, :].bitcast(I32), x_scales[0, r:16:2, :].bitcast(I32))
         nc.sync.dma_start(x_win[:].bitcast(I32), words_of(x_words))
         nc.sync.dma_start(w1_raw[:].bitcast(I32), words_of(w1_words))
         nc.sync.dma_start(w2_raw[:].bitcast(I32), words_of(w2_words))
-        nc.gpsimd.dma_start(gs_t[:], gs.rearrange("(p t) o -> p (t o)", t=PACK))
 
         def gather_packed(dst, window, offsets):
             nc.vector.tensor_copy(dst, window[:].indirect(offsets))
 
-        def place_scale_rows(got, width, name, queue):
+        def place_scale_rows(got, width, name, engine, queue, moves):
             plane = keep.tile([P, width], U8, name=name, tag=name, align_bytes=64)
-            nc.vector.tensor_copy(plane[:].bitcast(I32), got[:].bitcast(I32))
-            place_rows(plane, got, queue)
+            engine.tensor_copy(plane[:].bitcast(I32), got[:].bitcast(I32))
+            for to_row, from_row in moves:
+                queue.dma_start(plane[to_row:P:32, :].bitcast(I32), got[from_row:P:32, :].bitcast(I32))
             return plane
 
         tau_neg = keep.tile([P, PACK], F32, name="tau_neg")
@@ -82,23 +79,25 @@ def tile_picked_thcesdpagq_none_p_kernel(
         tok_bytes = keep.tile([P, 2 * S], U8, name="tok_bytes")
         gather_packed(tok_bytes[:, 0:S], xs_win, hz_l[:])
         gather_packed(tok_bytes[:, S : 2 * S], xs_win, offs_l[:])
-        tok_plane = place_scale_rows(tok_bytes, 2 * S, "tok_plane", nc.scalar)
+        tok_plane = place_scale_rows(tok_bytes, 2 * S, "tok_plane", nc.vector, nc.sync, X_MOVES)
 
         gs2 = keep.tile([P, PACK], F32, name="gs2")
         gs_half = keep.tile([P, PACK], F32, name="gs_half")
 
         ws_dealt = keep.tile([P, 2 * H], U8, name="ws_dealt")
-        w1 = keep.tile([P, PACK, P], U32, name="w1", tag="words_then_cand", align_bytes=64)
+        w1 = keep.tile([P, PACK, P], U32, name="w1", align_bytes=64)
         w2 = keep.tile([P, PACK, P], U32, name="w2", align_bytes=64)
 
         for i in range(2):
-            nc.vector.tensor_copy(
-                ws_dealt[:, i * H : (i + 1) * H].rearrange("p (t m) -> p m t", t=PACK),
-                ws_raw[:, i, :].rearrange("p (m t) -> p m t", t=PACK),
+            nc.gpsimd.tensor_copy(
+                ws_dealt[:, i * H : (i + 1) * H].rearrange("p (t m) -> p t m", t=PACK),
+                ws_raw[:, i, :].rearrange("p (m t) -> p t m", t=PACK),
             )
-        ws = place_scale_rows(ws_dealt, 2 * H, "bytes_then_cand", nc.sync)
+        ws = place_scale_rows(ws_dealt, 2 * H, "ws_plane", nc.gpsimd, nc.scalar, W_MOVES)
+        n1_l = load_list(n1, "n1_l")
         cand_l = load_list(cand, "cand_l")
         n2_l = load_list(n2, "n2_l")
+        nc.sync.dma_start(gs_t[:], gs.rearrange("(p t) o -> p (t o)", t=PACK))
         n5_l = load_list(n5, "n5_l")
         n3_l = load_list(n3, "n3_l")
         n4_l = load_list(n4, "n4_l")
@@ -133,7 +132,7 @@ def tile_picked_thcesdpagq_none_p_kernel(
             y = keep.tile([P, 2 * S], F32, name="y%d" % t)
             nc.vector.tensor_scalar(y[:, 0:S], acc[:], 1.0, None, ALU.mult, ALU.max, accum_out=top[:, t : t + 1])
             nc.vector.tensor_tensor(bias[:, t : t + 1], top[:, t : t + 1], tau_neg[:, t : t + 1], ALU.mult)
-            ea = keep.tile([P, S], F32, name="ea%d" % t)
+            ea = keep.tile([P, S], F32, name="ea%d" % t, tag="ea%d" % t, align_bytes=64)
             nc.scalar.activation(
                 ea[:], y[:].indirect(n1_l[:]), ACT.Exp, bias=bias[:, t : t + 1], scale=tau_t[:, t : t + 1]
             )
@@ -159,11 +158,11 @@ def tile_picked_thcesdpagq_none_p_kernel(
             yh = keep.tile([P, S], F32, name="yh%d" % t)
             nc.vector.tensor_scalar(yh[:], ys[t][:, 0:S], gs_half[:, t : t + 1], None, ALU.mult)
             yhs.append(yh)
-        cand_words = keep.tile([P, C], U32, name="cand_words", tag="words_then_cand", align_bytes=64)
-        cand_bytes = keep.tile([P, C], U8, name="cand_bytes", tag="bytes_then_cand", align_bytes=64)
+        cand_words = keep.tile([P, C], U32, name="cand_words", tag="ea3", align_bytes=64)
+        cand_bytes = keep.tile([P, C], U8, name="cand_bytes", tag="ea2", align_bytes=64)
         for lo in range(0, C, S):
             gather_packed(cand_bytes[:, lo : lo + S], xs_win, cand_l[:, lo // 16 : (lo + S) // 16])
-        cand_plane = place_scale_rows(cand_bytes, C, "cand_plane", nc.sync)
+        cand_plane = place_scale_rows(cand_bytes, C, "cand_plane", nc.vector, nc.sync, X_MOVES)
         for lo in range(0, C, S):
             gather_packed(cand_words[:, lo : lo + S], x_win, cand_l[:, lo // 16 : (lo + S) // 16])
         for t in range(PACK - 1):

from contextlib import ExitStack

import concourse.mybir as mybir

F32 = mybir.dt.float32
BF16 = mybir.dt.bfloat16
I32 = mybir.dt.int32
U32 = mybir.dt.uint32
U16 = mybir.dt.uint16
U8 = mybir.dt.uint8
FP8X4 = mybir.dt.float8_e4m3fn_x4
ALU = mybir.AluOpType
ACT = mybir.ActivationFunctionType

P = 128
PACK = 4
K, T, S, H, C, U = 512, 2048, 256, 512, 512, 512
HALF = S // 2
X_MOVES = ((2, 16), (3, 17))
W_MOVES = ((1, 8), (2, 16), (3, 24))
FLOPS = 2 * (2 * K * H * S + K * C * S)


def tile_picked_thcesdpagq_none_p_kernel(
    tc, x_words, x_scales, w1_words, w1_scales, w2_words, w2_scales, tau, gs, offs, hz, n1, n2, cand, n3, n4, n5, out
):
    nc = tc.nc
    with ExitStack() as ctx:
        lists = ctx.enter_context(tc.tile_pool(name="lists", bufs=1))
        keep = ctx.enter_context(tc.tile_pool(name="keep", bufs=1))
        psum = ctx.enter_context(tc.psum_pool(name="psum", bufs=1))

        def load_list(src, name):
            tile = lists.tile(list(src.shape), U16, name=name)
            nc.sync.dma_start(tile[:], src)
            return tile

        def words_of(src):
            return src[0].rearrange("p n t -> p (n t)").bitcast(I32)

        def bank(index, width):
            return psum.tile([P, width], F32, name="bank%d" % index, tag="bank%d" % index)

        xs_win = keep.tile([P, T], U8, name="xs_win")
        x_win = keep.tile([P, T], U32, name="x_win")
        w1_raw = keep.tile([P, H], U32, name="w1_raw")
        w2_raw = keep.tile([P, H], U32, name="w2_raw")
        ws_raw = keep.tile([P, 2, H], U8, name="ws_raw")
        tau_t = keep.tile([P, PACK], F32, name="tau_t")
        gs_t = keep.tile([P, PACK], F32, name="gs_t")
        nc.vector.memset(xs_win[:, 0 : T // 2].bitcast(I32), 0)
        nc.gpsimd.memset(xs_win[:, T // 2 : T].bitcast(I32), 0)

        hz_l = load_list(hz, "hz_l")
        nc.sync.dma_start(tau_t[:], tau.rearrange("(p t) o -> p (t o)", t=PACK))
        offs_l = load_list(offs, "offs_l")
        for i, src in enumerate((w1_scales, w2_scales)):
            rows = src[0].bitcast(I32).unsqueeze(1).broadcast_to([16, 8, H // 4])
            nc.scalar.dma_start(ws_raw[:, i, :].bitcast(I32), rows)
        for r, queue in enumerate((nc.sync, nc.scalar)):
            queue.dma_start(xs_win[r:P:16, :].bitcast(I32), x_scales[0, r:16:2, :].bitcast(I32))
        nc.sync.dma_start(x_win[:].bitcast(I32), words_of(x_words))
        nc.sync.dma_start(w1_raw[:].bitcast(I32), words_of(w1_words))
        nc.sync.dma_start(w2_raw[:].bitcast(I32), words_of(w2_words))

        def gather_packed(dst, window, offsets):
            nc.vector.tensor_copy(dst, window[:].indirect(offsets))

        def place_scale_rows(got, width, name, engine, queue, moves):
            plane = keep.tile([P, width], U8, name=name, tag=name, align_bytes=64)
            engine.tensor_copy(plane[:].bitcast(I32), got[:].bitcast(I32))
            for to_row, from_row in moves:
                queue.dma_start(plane[to_row:P:32, :].bitcast(I32), got[from_row:P:32, :].bitcast(I32))
            return plane

        tau_neg = keep.tile([P, PACK], F32, name="tau_neg")
        nc.scalar.activation(tau_neg[:], tau_t[:], ACT.Copy, scale=-1.0)

        tok_bytes = keep.tile([P, 2 * S], U8, name="tok_bytes")
        gather_packed(tok_bytes[:, 0:S], xs_win, hz_l[:])
        gather_packed(tok_bytes[:, S : 2 * S], xs_win, offs_l[:])
        tok_plane = place_scale_rows(tok_bytes, 2 * S, "tok_plane", nc.vector, nc.sync, X_MOVES)

        gs2 = keep.tile([P, PACK], F32, name="gs2")
        gs_half = keep.tile([P, PACK], F32, name="gs_half")

        ws_dealt = keep.tile([P, 2 * H], U8, name="ws_dealt")
        w1 = keep.tile([P, PACK, P], U32, name="w1", align_bytes=64)
        w2 = keep.tile([P, PACK, P], U32, name="w2", align_bytes=64)

        for i in range(2):
            nc.gpsimd.tensor_copy(
                ws_dealt[:, i * H : (i + 1) * H].rearrange("p (t m) -> p t m", t=PACK),
                ws_raw[:, i, :].rearrange("p (m t) -> p t m", t=PACK),
            )
        ws = place_scale_rows(ws_dealt, 2 * H, "ws_plane", nc.gpsimd, nc.scalar, W_MOVES)
        n1_l = load_list(n1, "n1_l")
        cand_l = load_list(cand, "cand_l")
        n2_l = load_list(n2, "n2_l")
        nc.sync.dma_start(gs_t[:], gs.rearrange("(p t) o -> p (t o)", t=PACK))
        n5_l = load_list(n5, "n5_l")
        n3_l = load_list(n3, "n3_l")
        n4_l = load_list(n4, "n4_l")

        def deal(copy, dealt, raw, lo, hi):
            copy(dealt[:].rearrange("p t m -> p m t")[:, lo:hi, :], raw[:].rearrange("p (m t) -> p m t", t=PACK)[:, lo:hi, :])

        deal(nc.scalar.copy, w1, w1_raw, 0, P)
        deal(nc.scalar.copy, w2, w2_raw, 0, P // 2)

        offs_words = keep.tile([P, S], U32, name="offs_words", align_bytes=64)
        hz_words = keep.tile([P, S], U32, name="hz_words", align_bytes=64)
        gather_packed(offs_words[:], x_win, offs_l[:])
        gather_packed(hz_words[:], x_win, hz_l[:])
        deal(nc.vector.tensor_copy, w2, w2_raw, P // 2, P)

        top = keep.tile([P, PACK], F32, name="top")
        bias = keep.tile([P, PACK], F32, name="bias")
        z = keep.tile([P, S, PACK], BF16, name="z", align_bytes=64)
        ys, eas, dss, yhs = [], [], [], []

        def project(t):
            acc = bank(t, S)
            nc.tensor.matmul_mx(
                out=acc[:], lhsT=w1[:, t, :].bitcast(FP8X4), lhsT_scale=ws[:, t * P : (t + 1) * P],
                rhs=offs_words[:].bitcast(FP8X4), rhs_scale=tok_plane[:, S : 2 * S], start=True, stop=False,
            )
            nc.tensor.matmul_mx(
                out=acc[:], lhsT=w2[:, t, :].bitcast(FP8X4), lhsT_scale=ws[:, H + t * P : H + (t + 1) * P],
                rhs=hz_words[:].bitcast(FP8X4), rhs_scale=tok_plane[:, 0:S], start=False, stop=True,
            )
            y = keep.tile([P, 2 * S], F32, name="y%d" % t)
            nc.vector.tensor_scalar(y[:, 0:S], acc[:], 1.0, None, ALU.mult, ALU.max, accum_out=top[:, t : t + 1])
            nc.vector.tensor_tensor(bias[:, t : t + 1], top[:, t : t + 1], tau_neg[:, t : t + 1], ALU.mult)
            ea = keep.tile([P, S], F32, name="ea%d" % t, tag="ea%d" % t, align_bytes=64)
            nc.scalar.activation(
                ea[:], y[:].indirect(n1_l[:]), ACT.Exp, bias=bias[:, t : t + 1], scale=tau_t[:, t : t + 1]
            )
            ys.append(y)
            eas.append(ea)

        def weigh(t, lo, hi):
            nc.vector.scalar_tensor_tensor(
                z[:, lo:hi, t], dss[t][:, lo:hi], gs2[:, t : t + 1], yhs[t][:, lo:hi], ALU.mult, ALU.add
            )

        for t in range(PACK):
            project(t)
        for t in range(PACK):
            sm = keep.tile([P, S], F32, name="sm%d" % t)
            nc.vector.tensor_tensor(sm[:], ys[t][:, 0:S], eas[t][:], ALU.mult)
            ds = keep.tile([P, 2 * S], F32, name="ds%d" % t)
            nc.scalar.activation(ds[:].indirect(n2_l[:]), sm[:], ACT.Copy)
            dss.append(ds)
        nc.gpsimd.tensor_scalar(gs2[:], gs_t[:], 2.0, None, ALU.mult)
        nc.gpsimd.tensor_scalar(gs_half[:], gs_t[:], -0.5, None, ALU.mult)
        for t in range(PACK):
            yh = keep.tile([P, S], F32, name="yh%d" % t)
            nc.vector.tensor_scalar(yh[:], ys[t][:, 0:S], gs_half[:, t : t + 1], None, ALU.mult)
            yhs.append(yh)
        cand_words = keep.tile([P, C], U32, name="cand_words", tag="ea3", align_bytes=64)
        cand_bytes = keep.tile([P, C], U8, name="cand_bytes", tag="ea2", align_bytes=64)
        for lo in range(0, C, S):
            gather_packed(cand_bytes[:, lo : lo + S], xs_win, cand_l[:, lo // 16 : (lo + S) // 16])
        cand_plane = place_scale_rows(cand_bytes, C, "cand_plane", nc.vector, nc.sync, X_MOVES)
        for lo in range(0, C, S):
            gather_packed(cand_words[:, lo : lo + S], x_win, cand_l[:, lo // 16 : (lo + S) // 16])
        for t in range(PACK - 1):
            weigh(t, 0, S)

        pages = []
        for c in range(C // P):
            page = keep.tile([P, U], F32, name="page%d" % c)
            pages.append(page)

        z_words = keep.tile([P, S], U32, name="z_words", align_bytes=64)
        z_plane = keep.tile([P, S], U8, name="z_plane", align_bytes=64)
        for lo in (0, HALF):
            weigh(PACK - 1, lo, lo + HALF)
        for lo in (0, HALF):
            nc.vector.quantize_mx(
                out=z_words[:, lo : lo + HALF].bitcast(FP8X4),
                scales=z_plane[:, lo : lo + HALF],
                in_=z[:, lo : lo + HALF, :].rearrange("p j t -> p (j t)"),
            )

        def score(acc, c, lo, hi):
            nc.tensor.matmul_mx(
                out=acc[:], lhsT=cand_words[:, c * P : (c + 1) * P].bitcast(FP8X4),
                lhsT_scale=cand_plane[:, c * P : (c + 1) * P],
                rhs=z_words[:, lo:hi].bitcast(FP8X4), rhs_scale=z_plane[:, lo:hi], start=True, stop=True,
            )

        news = []

        def finish(c):
            nc.scalar.activation(pages[c][:].indirect(n4_l[:]), news[c][:], ACT.Copy)
            nc.sync.dma_start(out[c * P : (c + 1) * P, :], pages[c][:])

        for c in range(C // P):
            s = keep.tile([P, S + 16], F32, name="s%d" % c)
            other = keep.tile([P, S], F32, name="other%d" % c)
            if c == 0:
                first, second = bank(4, HALF), bank(5, HALF)
                score(first, c, 0, HALF)
                score(second, c, HALF, S)
                nc.scalar.activation(s[:, 0:HALF], first[:], ACT.Copy, scale=0.0625)
                nc.scalar.activation(pages[c][:].indirect(n3_l[:, 0 : HALF // 16]), s[:, 0:HALF], ACT.Copy)
                nc.vector.tensor_scalar(s[:, HALF:S], second[:], 0.0625, None, ALU.mult)
                nc.scalar.activation(other[:], s[:].indirect(n5_l[:]), ACT.Copy)
                nc.scalar.activation(pages[c][:].indirect(n3_l[:, HALF // 16 : S // 16]), s[:, HALF:S], ACT.Copy)
            else:
                acc = bank((5 + c) % 8, S)
                score(acc, c, 0, S)
                nc.vector.tensor_scalar(s[:, 0:S], acc[:], 0.0625, None, ALU.mult)
                nc.scalar.activation(other[:], s[:].indirect(n5_l[:]), ACT.Copy)
                nc.scalar.activation(pages[c][:].indirect(n3_l[:]), s[:, 0:S], ACT.Copy)
            nw = keep.tile([P, S], F32, name="nw%d" % c)
            nc.vector.tensor_tensor(nw[:], s[:, 0:S], other[:], ALU.subtract)
            news.append(nw)
            finish(c)
